import numpy as np
import ml_dtypes


def mxq(x, axis, fmt="e4m3"):
    dtype, down = {"e4m3": (ml_dtypes.float8_e4m3fn, 7), "e5m2": (ml_dtypes.float8_e5m2, 14)}[fmt]
    v = np.moveaxis(np.asarray(x, np.float32).astype(ml_dtypes.bfloat16).astype(np.float64), axis, -1)
    blocks = v.reshape(v.shape[:-1] + (-1, 32))
    amax = np.abs(blocks).max(-1, keepdims=True)
    byte = np.maximum(np.where(amax > 0, np.frexp(amax)[1] - 1 + 127, 0) - down, 1)
    scale = np.exp2(byte - 127.0)
    codes = (blocks / scale).astype(np.float32).astype(dtype).astype(np.float64)
    return np.moveaxis((codes * scale).reshape(v.shape), -1, axis)


WIDE = False


def mx_kscale(k):
    if not WIDE:
        return np.ones(k)
    levels = np.array([10, -10, 5, -5, 0])
    if k % 512:
        return np.exp2(np.random.permutation(np.resize(levels, k // 32))).repeat(32)
    a = np.empty((k // 512, 16))
    for p in range(k // 512):
        a[p, :8] = np.random.permutation(np.resize(levels, 8))
        for g in range(8):
            far = levels[np.abs(levels - a[p, g]) >= 10]
            a[p, g + 8] = far[np.random.randint(len(far))]
    return np.exp2(a.ravel()).repeat(32)


def f64(x):
    return np.asarray(x).astype(np.float64)


def striped(idx):
    return np.tile(np.asarray(idx).reshape(-1, 16).T, (8, 1)).astype(np.uint16)


def unstriped(offs):
    return offs[:16].T.reshape(-1).astype(np.int64)


E2M1 = np.array([0.0, 0.5, 1.0, 1.5, 2.0, 3.0, 4.0, 6.0, -0.0, -0.5, -1.0, -1.5, -2.0, -3.0, -4.0, -6.0])


def pack_weight(w, fmt):
    k, n = w.shape
    w = f64(np.asarray(w, np.float32).astype(ml_dtypes.bfloat16)).reshape(k // 32, 32, n)
    amax = np.abs(w).max(1)
    if fmt == "e4m3":
        byte = np.frexp(amax)[1] - 1 + 127 - 7
    else:
        mant, ex = np.frexp(amax / 6.0)
        byte = np.where(mant > 0.5, ex, ex - 1) + 127
    byte = np.clip(np.where(amax > 0, byte, 1), 1, 254)
    scaled = (w * np.exp2(127.0 - byte)[:, None, :]).reshape(k, n).astype(np.float32)
    by_word = np.ascontiguousarray(scaled.reshape(k // 512, 128, 4, n).transpose(0, 1, 3, 2))
    if fmt == "e4m3":
        words = by_word.astype(ml_dtypes.float8_e4m3fn).view(np.uint8)
    else:
        c = by_word.astype(ml_dtypes.float4_e2m1fn).view(np.uint8) & 0xF
        words = (c[..., 0::2] | (c[..., 1::2] << 4)).reshape(k // 512, 128, 2 * n)
    return np.ascontiguousarray(words), np.ascontiguousarray(byte.astype(np.uint8).reshape(k // 512, 16, n))


def unpack_weight(words, scales, fmt):
    g, _, n = scales.shape
    words = np.ascontiguousarray(words).reshape(g, 128, n, -1)
    if fmt == "e4m3":
        vals = words.view(ml_dtypes.float8_e4m3fn).astype(np.float64)
    else:
        nib = np.empty((g, 128, n, 4), np.uint8)
        nib[..., 0::2] = words & 0xF
        nib[..., 1::2] = words >> 4
        vals = E2M1[nib]
    vals = vals * np.repeat(np.exp2(scales.astype(np.float64) - 127.0), 8, axis=1)[..., None]
    return vals.transpose(0, 1, 3, 2).reshape(g * 512, n)


D, E, T, I, Q = 512, 512, 2048, 512, 128


def setup_inputs():
    n = np.random.standard_normal
    idx = np.random.permutation(T)[:I]
    fd = mx_kscale(D)
    fi = mx_kscale(I)
    ti = np.ones(T)
    ti[idx] = fi
    keysp = pack_weight(n((D, T)) / fd[:, None], "e4m3")
    return {
        "query": (n((D, Q)) * 0.7 / np.sqrt(D) * fd[:, None]).astype(np.float32),
        "dquery": (n((D, Q)) * 1.0 / np.sqrt(D) * fd[:, None]).astype(np.float32),
        "query2": (n((D, Q)) * 0.7 / np.sqrt(D) * fd[:, None]).astype(np.float32),
        "dquery2": (n((D, Q)) * 1.0 / np.sqrt(D) * fd[:, None]).astype(np.float32),
        "keys_words": keysp[0],
        "keys_scales": keysp[1],
        "os": (np.random.uniform(8.0, 32.0, (1, I)) * fi).astype(np.float32),
        "vals": (n((E, T)) / ti).astype(np.float32),
        "offs": striped(idx),
    }


def reference(query, dquery, query2, dquery2, keys_words, keys_scales, os, vals, offs):
    idx = unstriped(offs)
    keysu = unpack_weight(keys_words, keys_scales, "e4m3")
    queryq = mxq(f64(query), 0, "e4m3")
    keysidxg = keysu[:, idx]
    a = queryq.T @ keysidxg
    dqueryq = mxq(f64(dquery), 0, "e4m3")
    ta = dqueryq.T @ keysidxg
    query2q = mxq(f64(query2), 0, "e4m3")
    b = query2q.T @ keysidxg
    dquery2q = mxq(f64(dquery2), 0, "e4m3")
    tb = dquery2q.T @ keysidxg
    pa = np.exp(a - np.max(a, axis=1, keepdims=True))
    wa = pa / np.sum(pa, axis=1, keepdims=True)
    pb = np.exp(b - np.max(b, axis=1, keepdims=True))
    wb = pb / np.sum(pb, axis=1, keepdims=True)
    tpa = ta * pa
    twa = (tpa - np.sum(tpa, axis=1, keepdims=True) * pa / np.sum(pa, axis=1, keepdims=True)) / np.sum(pa, axis=1, keepdims=True)
    tpb = tb * pb
    twb = (tpb - np.sum(tpb, axis=1, keepdims=True) * pb / np.sum(pb, axis=1, keepdims=True)) / np.sum(pb, axis=1, keepdims=True)
    tw = (twa * wb + twb * wa - (twa + twb) * wa * wb / (wa + wb)) / (wa + wb)
    wo1 = tw * f64(os)
    wt1 = wo1.T
    vt1 = f64(vals)[:, idx].T
    wt1q = mxq(wt1, 0, "e4m3")
    vt1q = mxq(vt1, 0, "e4m3")
    o = wt1q.T @ vt1q
    return o

@@ -1,0 +1,250 @@
+import math
+from contextlib import ExitStack
+
+import concourse.mybir as mybir
+from concourse.masks import make_identity
+
+F32 = mybir.dt.float32
+BF16 = mybir.dt.bfloat16
+I32 = mybir.dt.int32
+U32 = mybir.dt.uint32
+U16 = mybir.dt.uint16
+U8 = mybir.dt.uint8
+FP8X4 = mybir.dt.float8_e4m3fn_x4
+ALU = mybir.AluOpType
+ACT = mybir.ActivationFunctionType
+
+D, E, T, I, Q = 512, 512, 2048, 512, 128
+P = 128
+PACK = 4
+FLOPS = 2 * 4 * D * Q * I + 2 * I * Q * E
+
+LN_PER_BIT = math.log(2.0) / 2.0**23
+
+
+def tile_attend_ttagreement_kernel(tc, query, dquery, query2, dquery2, keys_words, keys_scales, slot_factor, vals, offs, out):
+    nc = tc.nc
+    with ExitStack() as ctx:
+        sb = ctx.enter_context(tc.tile_pool(name="sb", bufs=1))
+        ps = ctx.enter_context(tc.psum_pool(name="ps", bufs=1))
+
+        def col(name):
+            return sb.tile([P, 1], F32, name=name)
+
+        def wide(name, tag=""):
+            return sb.tile([P, I], F32, name=name, tag=tag, align_bytes=64)
+
+        def bank(tag, name):
+            return ps.tile([P, 512], F32, tag=tag, name=name)
+
+        def dealt(scores):
+            return scores.rearrange("q (s r) -> q r s", r=PACK)
+
+        def planes(t):
+            return t.rearrange("q (r s) -> q r s", r=PACK)
+
+        def woven(turned):
+            return turned.rearrange("s (r q) -> s q r", r=PACK)
+
+        def words4(t):
+            return t.rearrange("s (q r) -> s q r", r=PACK)
+
+        offsets = sb.tile([P, I // 16], U16, name="offsets")
+        nc.sync.dma_start(offsets[:], offs)
+
+        kscale_pool = sb.tile([P, T], U8, name="kscale_pool", align_bytes=64)
+        nc.gpsimd.memset(kscale_pool[:].bitcast(I32), 0)
+        os_cols = sb.tile([P, PACK], F32, name="os_cols")
+        nc.sync.dma_start(out=os_cols[:], in_=slot_factor.rearrange("o (p r) -> (o p) r", r=PACK))
+        kword_pool = sb.tile([P, T], I32, name="kword_pool", align_bytes=64)
+        nc.sync.dma_start(out=kword_pool[:], in_=keys_words[0].rearrange("p n t -> p (n t)").bitcast(I32))
+        raw = {}
+        raw["b"] = sb.tile([P, PACK, Q], F32, name="raw_b")
+        nc.sync.dma_start(out=raw["b"][:], in_=query2.rearrange("(p j) q -> p j q", j=PACK))
+        for quad in range(4):
+            nc.scalar.dma_start(
+                out=kscale_pool[32 * quad : 32 * quad + 4, :].bitcast(I32),
+                in_=keys_scales[0, 4 * quad : 4 * quad + 4, :].bitcast(I32),
+            )
+
+        minus_two = col("minus_two")
+        nc.gpsimd.memset(minus_two[:], -2.0)
+
+        ident = sb.tile([P, P], F32, name="ident")
+        make_identity(nc, ident[:])
+        for name, src in (("a", query), ("tb", dquery2), ("ta", dquery)):
+            raw[name] = sb.tile([P, PACK, Q], F32, name="raw_" + name)
+            nc.sync.dma_start(out=raw[name][:], in_=src.rearrange("(p j) q -> p j q", j=PACK))
+        vpool = []
+        for j in range(E // P):
+            vpool.append(sb.tile([P, T], F32, name="vpool%d" % j, tag="pool%d" % j, align_bytes=64))
+            nc.sync.dma_start(out=vpool[j][:], in_=vals[j * P : (j + 1) * P, :])
+
+        def turn(dst, src, first, last):
+            for r in range(PACK):
+                nc.tensor.matmul(
+                    dst[:, r * P : (r + 1) * P],
+                    lhsT=src(r),
+                    rhs=ident[:],
+                    is_transpose=True,
+                    start=(first and r == 0),
+                    stop=(last and r == PACK - 1),
+                )
+
+        def plane(t):
+            return lambda r: t[:, r * P : (r + 1) * P]
+
+        kscales = sb.tile([P, I], U8, name="kscales", align_bytes=64)
+        nc.vector.tensor_copy(kscales[:], kscale_pool[:].indirect(offsets[:]))
+        kwords = sb.tile([P, I], U32, name="kwords", align_bytes=64)
+        nc.vector.tensor_copy(kwords[:], kword_pool[:].bitcast(U32).indirect(offsets[:]))
+
+        score = {}
+        for name in ("b", "a", "tb", "ta"):
+            grouped = sb.tile([P, Q * PACK], BF16, name="grouped_" + name, align_bytes=64)
+            nc.scalar.activation(out=words4(grouped[:]), in_=raw[name][:].rearrange("p j q -> p q j"), func=ACT.Copy)
+            codes = sb.tile([P, Q], U32, name="codes_" + name, align_bytes=64)
+            scales = sb.tile([P, Q], U8, name="scales_" + name, align_bytes=64)
+            nc.vector.quantize_mx(out=codes[:].bitcast(FP8X4), scales=scales[:], in_=grouped[:])
+            score[name] = bank("bank_" + name, "score_" + name)
+            nc.tensor.matmul_mx(
+                out=score[name][:],
+                lhsT=codes[:].bitcast(FP8X4),
+                lhsT_scale=scales[:],
+                rhs=kwords[:].bitcast(FP8X4),
+                rhs_scale=kscales[:],
+                start=True,
+                stop=True,
+            )
+
+        neg_b, neg_max_b = wide("neg_b"), col("neg_max_b")
+        nc.vector.tensor_scalar(planes(neg_b[:]), dealt(score["b"][:]), -1.0, None, ALU.mult, ALU.min, accum_out=neg_max_b[:])
+        pb, sum_b = wide("pb"), col("sum_b")
+        nc.scalar.activation(out=planes(pb[:]), in_=dealt(score["b"][:]), func=ACT.Exp, bias=neg_max_b[:], accum_out=sum_b[:])
+        copy_a, max_a, neg_max_a = wide("copy_a"), col("max_a"), col("neg_max_a")
+        nc.vector.tensor_scalar(planes(copy_a[:]), dealt(score["a"][:]), 1.0, None, ALU.mult, ALU.max, accum_out=max_a[:])
+        nc.vector.tensor_scalar(neg_max_a[:], max_a[:], -1.0, None, ALU.mult)
+        pa, sum_a = wide("pa", "then_values1"), col("sum_a")
+        nc.scalar.activation(out=pa[:], in_=score["a"][:], func=ACT.Exp, bias=neg_max_a[:], accum_out=sum_a[:])
+
+        rb, neg_rb, neg_rb2, shift1 = col("rb"), col("neg_rb"), col("neg_rb2"), col("shift1")
+        nc.vector.tensor_scalar(shift1[:], neg_max_a[:], neg_max_b[:], 0.5, ALU.subtract, ALU.subtract)
+        nc.vector.reciprocal(rb[:], sum_b[:])
+        guess_b, guess_b_half = col("guess_b"), col("guess_b_half")
+        nc.vector.tensor_scalar(guess_b[:], sum_b[:].bitcast(I32), LN_PER_BIT, None, ALU.mult)
+        nc.vector.tensor_scalar(guess_b_half[:], sum_b[:].bitcast(I32), LN_PER_BIT, -0.5, ALU.mult, ALU.add)
+        nc.vector.tensor_scalar(neg_rb2[:], rb[:], rb[:], -1.0, ALU.mult, ALU.mult)
+        nc.vector.tensor_scalar(neg_rb[:], rb[:], -1.0, None, ALU.mult)
+        prod_b, bias_v = wide("prod_b"), col("bias_v")
+        nc.vector.scalar_tensor_tensor(
+            planes(prod_b[:]), dealt(score["tb"][:]), neg_rb2[:], planes(pb[:]), ALU.mult, ALU.mult, accum_out=bias_v[:]
+        )
+        ra = col("ra")
+        ra_rb = sb.tile([P, 1], F32, name="ra_rb", tag="then_values2", align_bytes=64)
+        nc.vector.reciprocal(ra[:], sum_a[:])
+        nc.vector.tensor_scalar(ra_rb[:], ra[:], rb[:], None, ALU.mult)
+        prod_a, bias_u = wide("prod_a", "then_values0"), col("bias_u")
+        nc.vector.scalar_tensor_tensor(prod_a[:], score["ta"][:], ra_rb[:], pa[:], ALU.mult, ALU.mult, accum_out=bias_u[:])
+
+        ratio, square2 = col("ratio"), col("square2")
+        e1, z0_half, square, z0_shift, e2, z1_shift, row_shift = (
+            col("e1"), col("z0_half"), col("square"), col("z0_shift"), col("e2"), col("z1_shift"), col("row_shift"))
+        bits = sum_a[:].bitcast(U32)
+        nc.scalar.activation(out=e1[:], in_=bits, func=ACT.Exp, scale=-LN_PER_BIT, bias=guess_b[:])
+        nc.scalar.activation(out=ratio[:], in_=sum_a[:], func=ACT.Copy, scale=rb[:])
+        nc.scalar.activation(out=z0_half[:], in_=bits, func=ACT.Identity, scale=-LN_PER_BIT, bias=guess_b_half[:])
+        nc.scalar.activation(out=square[:], in_=e1[:], func=ACT.Square, scale=ratio[:], bias=minus_two[:])
+        nc.scalar.activation(out=z0_shift[:], in_=z0_half[:], func=ACT.Identity, bias=shift1[:])
+        nc.scalar.activation(out=e2[:], in_=square[:], func=ACT.Exp, scale=0.5, bias=z0_half[:])
+        nc.scalar.activation(out=z1_shift[:], in_=square[:], func=ACT.Identity, scale=0.5, bias=z0_shift[:])
+        nc.scalar.activation(out=square2[:], in_=e2[:], func=ACT.Square, scale=ratio[:], bias=minus_two[:])
+        nc.scalar.activation(out=row_shift[:], in_=square2[:], func=ACT.Identity, scale=0.5, bias=z1_shift[:])
+
+        v, neg_u = wide("v"), wide("neg_u")
+        nc.scalar.activation(out=planes(v[:]), in_=dealt(score["tb"][:]), func=ACT.Identity, scale=rb[:], bias=bias_v[:])
+        nc.scalar.activation(out=planes(neg_u[:]), in_=dealt(score["ta"][:]), func=ACT.Identity, scale=neg_rb[:], bias=bias_u[:])
+
+        pb_t = bank("bank_b", "pb_t")
+        turn(pb_t, plane(pb), True, True)
+        pb_os = wide("pb_os")
+        for r in range(PACK):
+            nc.scalar.activation(out=plane(pb_os)(r), in_=plane(pb_t)(r), func=ACT.Copy, scale=os_cols[:, r : r + 1])
+        logit_t = bank("bank_a", "logit_t")
+        turn(logit_t, plane(neg_b), True, False)
+        turn(logit_t, plane(copy_a), False, False)
+        turn(logit_t, lambda r: row_shift[:, 0:1].to_broadcast([P, P]), False, True)
+        diff_t = bank("bank_diff", "diff_t")
+        turn(diff_t, plane(v), True, False)
+        turn(diff_t, plane(neg_u), False, True)
+        neg_u_t = bank("bank_u", "neg_u_t")
+        turn(neg_u_t, plane(neg_u), True, True)
+
+        def gather_values(j):
+            picked = sb.tile([P, I], BF16, name="picked%d" % j, tag="then_values%d" % j, align_bytes=64)
+            nc.vector.tensor_copy(picked[:], vpool[j][:].indirect(offsets[:]))
+            return picked
+
+        def turn_values(blocks, tag):
+            n = len(blocks)
+            turned = ps.tile([P, n, 2, P], F32, tag=tag, name="turned")
+            for k, picked in enumerate(blocks):
+                pairs = picked[:].bitcast(F32)
+                for u in range(2):
+                    nc.tensor.transpose(turned[:, k, u, :], pairs[:, u : I // 2 : 2], ident[:])
+            grouped_v = sb.tile([P, n * P * PACK], BF16, name="grouped_" + tag, align_bytes=64)
+            nc.scalar.copy(
+                out=grouped_v[:].bitcast(F32).rearrange("s (k e u) -> s k e u", k=n, u=2),
+                in_=turned[:].rearrange("s k u e -> s k e u"),
+            )
+            return grouped_v
+
+        def quantise(grouped, codes, scales):
+            nc.vector.quantize_mx(out=codes.bitcast(FP8X4), scales=scales, in_=grouped[:])
+
+        def mx_tiles(name, width):
+            return (
+                sb.tile([P, width], U32, name="codes_" + name, align_bytes=64),
+                sb.tile([P, width], U8, name="scales_" + name, align_bytes=64),
+            )
+
+        picked0 = gather_values(0)
+        picked1 = gather_values(1)
+        picked2 = gather_values(2)
+
+        share = wide("share", "then_values3")
+        nc.scalar.activation(out=words4(share[:]), in_=woven(logit_t[:]), func=ACT.Sigmoid)
+        g01 = turn_values([picked0, picked1], "bank_a")
+        g2 = turn_values([picked2], "bank_v2")
+        mix, change, harmonic = wide("mix", "pool2"), wide("change", "pool3"), wide("harmonic")
+        nc.vector.tensor_tensor(words4(mix[:]), woven(diff_t[:]), words4(share[:]), ALU.mult)
+        nc.vector.tensor_tensor(words4(harmonic[:]), woven(pb_os[:]), words4(share[:]), ALU.mult)
+        g3 = turn_values([gather_values(3)], "bank_v3")
+        nc.vector.tensor_tensor(words4(change[:]), words4(mix[:]), woven(neg_u_t[:]), ALU.subtract)
+        vcodes01, vscales01 = mx_tiles("v01", 2 * P)
+        vcodes23, vscales23 = mx_tiles("v23", 2 * P)
+        wcodes, wscales = mx_tiles("w", Q)
+        quantise(g01, vcodes01[:], vscales01[:])
+        weights = sb.tile([P, Q * PACK], BF16, name="weights", align_bytes=64)
+        nc.vector.tensor_tensor(weights[:], change[:], harmonic[:], ALU.mult)
+        quantise(g2, vcodes23[:, 0:P], vscales23[:, 0:P])
+        quantise(weights, wcodes[:], wscales[:])
+        quantise(g3, vcodes23[:, P : 2 * P], vscales23[:, P : 2 * P])
+
+        for tag, first, codes, scales in (("bank_tb", 0, vcodes01, vscales01), ("bank_ta", 2 * P, vcodes23, vscales23)):
+            acc = bank(tag, "acc%d" % first)
+            nc.tensor.matmul_mx(
+                out=acc[:, 0 : 2 * P],
+                lhsT=wcodes[:].bitcast(FP8X4),
+                lhsT_scale=wscales[:],
+                rhs=codes[:].bitcast(FP8X4),
+                rhs_scale=scales[:],
+                start=True,
+                stop=True,
+            )
+            result = sb.tile([P, 2 * P], F32, name="result%d" % first)
+            if first == 0:
+                nc.scalar.copy(out=result[:], in_=acc[:, 0 : 2 * P])
+                nc.scalar.dma_start(out=out[:, first : first + 2 * P], in_=result[:])
+            else:
+                nc.vector.tensor_copy(out=result[:], in_=acc[:, 0 : 2 * P])
+                nc.sync.dma_start(out=out[:, first : first + 2 * P], in_=result[:])

@@ -53,28 +53,28 @@ def tile_attend_ttagreement_kernel(tc, query, dquery, query2, dquery2, keys_word
         nc.sync.dma_start(offsets[:], offs)
 
         kscale_pool = sb.tile([P, T], U8, name="kscale_pool", align_bytes=64)
-        nc.gpsimd.memset(kscale_pool[:].bitcast(I32), 0)
-        os_cols = sb.tile([P, PACK], F32, name="os_cols")
-        nc.sync.dma_start(out=os_cols[:], in_=slot_factor.rearrange("o (p r) -> (o p) r", r=PACK))
-        kword_pool = sb.tile([P, T], I32, name="kword_pool", align_bytes=64)
-        nc.sync.dma_start(out=kword_pool[:], in_=keys_words[0].rearrange("p n t -> p (n t)").bitcast(I32))
+        nc.vector.memset(kscale_pool[:, 0 : T // 2].bitcast(I32), 0)
+        nc.gpsimd.memset(kscale_pool[:, T // 2 : T].bitcast(I32), 0)
         raw = {}
         raw["b"] = sb.tile([P, PACK, Q], F32, name="raw_b")
         nc.sync.dma_start(out=raw["b"][:], in_=query2.rearrange("(p j) q -> p j q", j=PACK))
         for quad in range(4):
-            nc.scalar.dma_start(
+            nc.sync.dma_start(
                 out=kscale_pool[32 * quad : 32 * quad + 4, :].bitcast(I32),
                 in_=keys_scales[0, 4 * quad : 4 * quad + 4, :].bitcast(I32),
             )
-
+        kword_pool = sb.tile([P, T], I32, name="kword_pool", align_bytes=64)
+        nc.sync.dma_start(out=kword_pool[:], in_=keys_words[0].rearrange("p n t -> p (n t)").bitcast(I32))
         minus_two = col("minus_two")
         nc.gpsimd.memset(minus_two[:], -2.0)
 
         ident = sb.tile([P, P], F32, name="ident")
         make_identity(nc, ident[:])
         for name, src in (("a", query), ("tb", dquery2), ("ta", dquery)):
-            raw[name] = sb.tile([P, PACK, Q], F32, name="raw_" + name)
+            raw[name] = sb.tile([P, PACK, Q], F32, name="raw_" + name, tag="raw_" + name, align_bytes=64)
             nc.sync.dma_start(out=raw[name][:], in_=src.rearrange("(p j) q -> p j q", j=PACK))
+        os_cols = sb.tile([P, PACK], F32, name="os_cols")
+        nc.sync.dma_start(out=os_cols[:], in_=slot_factor.rearrange("o (p r) -> (o p) r", r=PACK))
         vpool = []
         for j in range(E // P):
             vpool.append(sb.tile([P, T], F32, name="vpool%d" % j, tag="pool%d" % j, align_bytes=64))
@@ -100,12 +100,15 @@ def tile_attend_ttagreement_kernel(tc, query, dquery, query2, dquery2, keys_word
         nc.vector.tensor_copy(kwords[:], kword_pool[:].bitcast(U32).indirect(offsets[:]))
 
         score = {}
+        grouped = {}
         for name in ("b", "a", "tb", "ta"):
-            grouped = sb.tile([P, Q * PACK], BF16, name="grouped_" + name, align_bytes=64)
-            nc.scalar.activation(out=words4(grouped[:]), in_=raw[name][:].rearrange("p j q -> p q j"), func=ACT.Copy)
+            grouped[name] = sb.tile([P, Q * PACK], BF16, name="grouped_" + name, tag="grouped_" + name, align_bytes=64)
+            nc.scalar.activation(out=words4(grouped[name][:]), in_=raw[name][:].rearrange("p j q -> p q j"), func=ACT.Copy)
+
+        def scores(name):
             codes = sb.tile([P, Q], U32, name="codes_" + name, align_bytes=64)
             scales = sb.tile([P, Q], U8, name="scales_" + name, align_bytes=64)
-            nc.vector.quantize_mx(out=codes[:].bitcast(FP8X4), scales=scales[:], in_=grouped[:])
+            nc.vector.quantize_mx(out=codes[:].bitcast(FP8X4), scales=scales[:], in_=grouped[name][:])
             score[name] = bank("bank_" + name, "score_" + name)
             nc.tensor.matmul_mx(
                 out=score[name][:],
@@ -117,34 +120,38 @@ def tile_attend_ttagreement_kernel(tc, query, dquery, query2, dquery2, keys_word
                 stop=True,
             )
 
-        neg_b, neg_max_b = wide("neg_b"), col("neg_max_b")
-        nc.vector.tensor_scalar(planes(neg_b[:]), dealt(score["b"][:]), -1.0, None, ALU.mult, ALU.min, accum_out=neg_max_b[:])
-        pb, sum_b = wide("pb"), col("sum_b")
+        scores("b")
+        scores("a")
+        scores("tb")
+        copies = sb.tile([P, 2, I], F32, name="copies", tag="grouped_tb", align_bytes=64)
+        neg_b, copy_a = copies[:, 0, :], copies[:, 1, :]
+        neg_max_b = col("neg_max_b")
+        nc.vector.tensor_scalar(planes(neg_b), dealt(score["b"][:]), -1.0, None, ALU.mult, ALU.min, accum_out=neg_max_b[:])
+        pb, sum_b = wide("pb", "raw_ta"), col("sum_b")
         nc.scalar.activation(out=planes(pb[:]), in_=dealt(score["b"][:]), func=ACT.Exp, bias=neg_max_b[:], accum_out=sum_b[:])
-        copy_a, max_a, neg_max_a = wide("copy_a"), col("max_a"), col("neg_max_a")
-        nc.vector.tensor_scalar(planes(copy_a[:]), dealt(score["a"][:]), 1.0, None, ALU.mult, ALU.max, accum_out=max_a[:])
+        scores("ta")
+        max_a, neg_max_a = col("max_a"), col("neg_max_a")
+        nc.vector.tensor_scalar(planes(copy_a), dealt(score["a"][:]), 1.0, None, ALU.mult, ALU.max, accum_out=max_a[:])
         nc.vector.tensor_scalar(neg_max_a[:], max_a[:], -1.0, None, ALU.mult)
         pa, sum_a = wide("pa", "then_values1"), col("sum_a")
         nc.scalar.activation(out=pa[:], in_=score["a"][:], func=ACT.Exp, bias=neg_max_a[:], accum_out=sum_a[:])
 
-        rb, neg_rb, neg_rb2, shift1 = col("rb"), col("neg_rb"), col("neg_rb2"), col("shift1")
-        nc.vector.tensor_scalar(shift1[:], neg_max_a[:], neg_max_b[:], 0.5, ALU.subtract, ALU.subtract)
+        shift1, rb, guess_b, guess_b_half, ra = col("shift1"), col("rb"), col("guess_b"), col("guess_b_half"), col("ra")
         nc.vector.reciprocal(rb[:], sum_b[:])
-        guess_b, guess_b_half = col("guess_b"), col("guess_b_half")
         nc.vector.tensor_scalar(guess_b[:], sum_b[:].bitcast(I32), LN_PER_BIT, None, ALU.mult)
         nc.vector.tensor_scalar(guess_b_half[:], sum_b[:].bitcast(I32), LN_PER_BIT, -0.5, ALU.mult, ALU.add)
+        nc.vector.tensor_scalar(shift1[:], neg_max_a[:], neg_max_b[:], 0.5, ALU.subtract, ALU.subtract)
+        prod_b, tsum_b = wide("prod_b"), col("tsum_b")
+        nc.vector.scalar_tensor_tensor(
+            planes(prod_b[:]), dealt(score["tb"][:]), 1.0, planes(pb[:]), ALU.mult, ALU.mult, accum_out=tsum_b[:]
+        )
+        neg_rb, neg_rb2, ra_rb = col("neg_rb"), col("neg_rb2"), col("ra_rb")
         nc.vector.tensor_scalar(neg_rb2[:], rb[:], rb[:], -1.0, ALU.mult, ALU.mult)
         nc.vector.tensor_scalar(neg_rb[:], rb[:], -1.0, None, ALU.mult)
-        prod_b, bias_v = wide("prod_b"), col("bias_v")
-        nc.vector.scalar_tensor_tensor(
-            planes(prod_b[:]), dealt(score["tb"][:]), neg_rb2[:], planes(pb[:]), ALU.mult, ALU.mult, accum_out=bias_v[:]
-        )
-        ra = col("ra")
-        ra_rb = sb.tile([P, 1], F32, name="ra_rb", tag="then_values2", align_bytes=64)
         nc.vector.reciprocal(ra[:], sum_a[:])
+        prod_a, tsum_a = wide("prod_a", "then_values0"), col("tsum_a")
+        nc.vector.scalar_tensor_tensor(prod_a[:], score["ta"][:], 1.0, pa[:], ALU.mult, ALU.mult, accum_out=tsum_a[:])
         nc.vector.tensor_scalar(ra_rb[:], ra[:], rb[:], None, ALU.mult)
-        prod_a, bias_u = wide("prod_a", "then_values0"), col("bias_u")
-        nc.vector.scalar_tensor_tensor(prod_a[:], score["ta"][:], ra_rb[:], pa[:], ALU.mult, ALU.mult, accum_out=bias_u[:])
 
         ratio, square2 = col("ratio"), col("square2")
         e1, z0_half, square, z0_shift, e2, z1_shift, row_shift = (
@@ -160,15 +167,14 @@ def tile_attend_ttagreement_kernel(tc, query, dquery, query2, dquery2, keys_word
         nc.scalar.activation(out=square2[:], in_=e2[:], func=ACT.Square, scale=ratio[:], bias=minus_two[:])
         nc.scalar.activation(out=row_shift[:], in_=square2[:], func=ACT.Identity, scale=0.5, bias=z1_shift[:])
 
-        v, neg_u = wide("v"), wide("neg_u")
+        v, neg_u, bias_v, bias_u = wide("v"), wide("neg_u"), col("bias_v"), col("bias_u")
+        nc.scalar.activation(out=bias_v[:], in_=tsum_b[:], func=ACT.Copy, scale=neg_rb2[:])
+        nc.scalar.activation(out=bias_u[:], in_=tsum_a[:], func=ACT.Copy, scale=ra_rb[:])
         nc.scalar.activation(out=planes(v[:]), in_=dealt(score["tb"][:]), func=ACT.Identity, scale=rb[:], bias=bias_v[:])
         nc.scalar.activation(out=planes(neg_u[:]), in_=dealt(score["ta"][:]), func=ACT.Identity, scale=neg_rb[:], bias=bias_u[:])
 
         pb_t = bank("bank_b", "pb_t")
         turn(pb_t, plane(pb), True, True)
-        pb_os = wide("pb_os")
-        for r in range(PACK):
-            nc.scalar.activation(out=plane(pb_os)(r), in_=plane(pb_t)(r), func=ACT.Copy, scale=os_cols[:, r : r + 1])
         logit_t = bank("bank_a", "logit_t")
         turn(logit_t, plane(neg_b), True, False)
         turn(logit_t, plane(copy_a), False, False)
@@ -179,8 +185,8 @@ def tile_attend_ttagreement_kernel(tc, query, dquery, query2, dquery2, keys_word
         neg_u_t = bank("bank_u", "neg_u_t")
         turn(neg_u_t, plane(neg_u), True, True)
 
-        def gather_values(j):
-            picked = sb.tile([P, I], BF16, name="picked%d" % j, tag="then_values%d" % j, align_bytes=64)
+        def gather_values(j, tag):
+            picked = sb.tile([P, I], BF16, name="picked%d" % j, tag=tag, align_bytes=64)
             nc.vector.tensor_copy(picked[:], vpool[j][:].indirect(offsets[:]))
             return picked
 
@@ -207,33 +213,36 @@ def tile_attend_ttagreement_kernel(tc, query, dquery, query2, dquery2, keys_word
                 sb.tile([P, width], U8, name="scales_" + name, align_bytes=64),
             )
 
-        picked0 = gather_values(0)
-        picked1 = gather_values(1)
-        picked2 = gather_values(2)
+        picked0 = gather_values(0, "then_values0")
+        picked1 = gather_values(1, "then_values1")
+        picked2 = gather_values(2, "pool1")
 
-        share = wide("share", "then_values3")
+        share = wide("share")
         nc.scalar.activation(out=words4(share[:]), in_=woven(logit_t[:]), func=ACT.Sigmoid)
+        share_os = wide("share_os", "then_values3")
+        for r in range(PACK):
+            nc.scalar.activation(
+                out=plane(share_os)(r), in_=words4(share[:])[:, :, r], func=ACT.Copy, scale=os_cols[:, r : r + 1]
+            )
         g01 = turn_values([picked0, picked1], "bank_a")
-        g2 = turn_values([picked2], "bank_v2")
-        mix, change, harmonic = wide("mix", "pool2"), wide("change", "pool3"), wide("harmonic")
+        mix, change, harmonic = wide("mix", "pool2"), wide("change"), wide("harmonic")
         nc.vector.tensor_tensor(words4(mix[:]), woven(diff_t[:]), words4(share[:]), ALU.mult)
-        nc.vector.tensor_tensor(words4(harmonic[:]), woven(pb_os[:]), words4(share[:]), ALU.mult)
-        g3 = turn_values([gather_values(3)], "bank_v3")
+        g2 = turn_values([picked2], "bank_diff")
         nc.vector.tensor_tensor(words4(change[:]), words4(mix[:]), woven(neg_u_t[:]), ALU.subtract)
-        vcodes01, vscales01 = mx_tiles("v01", 2 * P)
-        vcodes23, vscales23 = mx_tiles("v23", 2 * P)
+        nc.vector.tensor_tensor(words4(harmonic[:]), woven(pb_t[:]), woven(share_os[:]), ALU.mult)
+        g3 = turn_values([gather_values(3, "then_values3")], "bank_u")
+        vmx = [mx_tiles("v01", 2 * P), mx_tiles("v2", P), mx_tiles("v3", P)]
         wcodes, wscales = mx_tiles("w", Q)
-        quantise(g01, vcodes01[:], vscales01[:])
-        weights = sb.tile([P, Q * PACK], BF16, name="weights", align_bytes=64)
+        quantise(g01, vmx[0][0][:], vmx[0][1][:])
+        quantise(g2, vmx[1][0][:], vmx[1][1][:])
+        weights = sb.tile([P, Q * PACK], BF16, name="weights", tag="pool3", align_bytes=64)
         nc.vector.tensor_tensor(weights[:], change[:], harmonic[:], ALU.mult)
-        quantise(g2, vcodes23[:, 0:P], vscales23[:, 0:P])
+        quantise(g3, vmx[2][0][:], vmx[2][1][:])
         quantise(weights, wcodes[:], wscales[:])
-        quantise(g3, vcodes23[:, P : 2 * P], vscales23[:, P : 2 * P])
 
-        for tag, first, codes, scales in (("bank_tb", 0, vcodes01, vscales01), ("bank_ta", 2 * P, vcodes23, vscales23)):
-            acc = bank(tag, "acc%d" % first)
+        def product(acc, codes, scales):
             nc.tensor.matmul_mx(
-                out=acc[:, 0 : 2 * P],
+                out=acc,
                 lhsT=wcodes[:].bitcast(FP8X4),
                 lhsT_scale=wscales[:],
                 rhs=codes[:].bitcast(FP8X4),
@@ -241,10 +250,15 @@ def tile_attend_ttagreement_kernel(tc, query, dquery, query2, dquery2, keys_word
                 start=True,
                 stop=True,
             )
-            result = sb.tile([P, 2 * P], F32, name="result%d" % first)
-            if first == 0:
-                nc.scalar.copy(out=result[:], in_=acc[:, 0 : 2 * P])
-                nc.scalar.dma_start(out=out[:, first : first + 2 * P], in_=result[:])
-            else:
-                nc.vector.tensor_copy(out=result[:], in_=acc[:, 0 : 2 * P])
-                nc.sync.dma_start(out=out[:, first : first + 2 * P], in_=result[:])
+
+        acc_first = bank("bank_tb", "acc_first")
+        product(acc_first[:, 0 : 2 * P], *vmx[0])
+        product(acc_first[:, 2 * P : 3 * P], *vmx[1])
+        result_first = sb.tile([P, 3 * P], F32, name="result_first")
+        nc.scalar.copy(out=result_first[:], in_=acc_first[:, 0 : 3 * P])
+        nc.scalar.dma_start(out=out[:, 0 : 3 * P], in_=result_first[:])
+        acc_last = bank("bank_ta", "acc_last")
+        product(acc_last[:, 0:P], *vmx[2])
+        result_last = sb.tile([P, P], F32, name="result_last")
+        nc.vector.tensor_copy(out=result_last[:], in_=acc_last[:, 0:P])
+        nc.sync.dma_start(out=out[:, 3 * P : 4 * P], in_=result_last[:])

import math
from contextlib import ExitStack

import concourse.mybir as mybir
from concourse.masks import make_identity

F32 = mybir.dt.float32
BF16 = mybir.dt.bfloat16
I32 = mybir.dt.int32
U32 = mybir.dt.uint32
U16 = mybir.dt.uint16
U8 = mybir.dt.uint8
FP8X4 = mybir.dt.float8_e4m3fn_x4
ALU = mybir.AluOpType
ACT = mybir.ActivationFunctionType

D, E, T, I, Q = 512, 512, 2048, 512, 128
P = 128
PACK = 4
FLOPS = 2 * 4 * D * Q * I + 2 * I * Q * E

LN_PER_BIT = math.log(2.0) / 2.0**23


def tile_attend_ttagreement_kernel(tc, query, dquery, query2, dquery2, keys_words, keys_scales, slot_factor, vals, offs, out):
    nc = tc.nc
    with ExitStack() as ctx:
        sb = ctx.enter_context(tc.tile_pool(name="sb", bufs=1))
        ps = ctx.enter_context(tc.psum_pool(name="ps", bufs=1))

        def col(name):
            return sb.tile([P, 1], F32, name=name)

        def wide(name, tag=""):
            return sb.tile([P, I], F32, name=name, tag=tag, align_bytes=64)

        def bank(tag, name):
            return ps.tile([P, 512], F32, tag=tag, name=name)

        def dealt(scores):
            return scores.rearrange("q (s r) -> q r s", r=PACK)

        def planes(t):
            return t.rearrange("q (r s) -> q r s", r=PACK)

        def woven(turned):
            return turned.rearrange("s (r q) -> s q r", r=PACK)

        def words4(t):
            return t.rearrange("s (q r) -> s q r", r=PACK)

        offsets = sb.tile([P, I // 16], U16, name="offsets")
        nc.sync.dma_start(offsets[:], offs)

        kscale_pool = sb.tile([P, T], U8, name="kscale_pool", align_bytes=64)
        nc.vector.memset(kscale_pool[:, 0 : T // 2].bitcast(I32), 0)
        nc.gpsimd.memset(kscale_pool[:, T // 2 : T].bitcast(I32), 0)
        raw = {}
        raw["b"] = sb.tile([P, PACK, Q], F32, name="raw_b")
        nc.sync.dma_start(out=raw["b"][:], in_=query2.rearrange("(p j) q -> p j q", j=PACK))
        for quad in range(4):
            nc.sync.dma_start(
                out=kscale_pool[32 * quad : 32 * quad + 4, :].bitcast(I32),
                in_=keys_scales[0, 4 * quad : 4 * quad + 4, :].bitcast(I32),
            )
        kword_pool = sb.tile([P, T], I32, name="kword_pool", align_bytes=64)
        nc.sync.dma_start(out=kword_pool[:], in_=keys_words[0].rearrange("p n t -> p (n t)").bitcast(I32))
        minus_two = col("minus_two")
        nc.gpsimd.memset(minus_two[:], -2.0)

        ident = sb.tile([P, P], F32, name="ident")
        make_identity(nc, ident[:])
        for name, src in (("a", query), ("tb", dquery2), ("ta", dquery)):
            raw[name] = sb.tile([P, PACK, Q], F32, name="raw_" + name, tag="raw_" + name, align_bytes=64)
            nc.sync.dma_start(out=raw[name][:], in_=src.rearrange("(p j) q -> p j q", j=PACK))
        os_cols = sb.tile([P, PACK], F32, name="os_cols")
        nc.sync.dma_start(out=os_cols[:], in_=slot_factor.rearrange("o (p r) -> (o p) r", r=PACK))
        vpool = []
        for j in range(E // P):
            vpool.append(sb.tile([P, T], F32, name="vpool%d" % j, tag="pool%d" % j, align_bytes=64))
            nc.sync.dma_start(out=vpool[j][:], in_=vals[j * P : (j + 1) * P, :])

        def turn(dst, src, first, last):
            for r in range(PACK):
                nc.tensor.matmul(
                    dst[:, r * P : (r + 1) * P],
                    lhsT=src(r),
                    rhs=ident[:],
                    is_transpose=True,
                    start=(first and r == 0),
                    stop=(last and r == PACK - 1),
                )

        def plane(t):
            return lambda r: t[:, r * P : (r + 1) * P]

        kscales = sb.tile([P, I], U8, name="kscales", align_bytes=64)
        nc.vector.tensor_copy(kscales[:], kscale_pool[:].indirect(offsets[:]))
        kwords = sb.tile([P, I], U32, name="kwords", align_bytes=64)
        nc.vector.tensor_copy(kwords[:], kword_pool[:].bitcast(U32).indirect(offsets[:]))

        score = {}
        grouped = {}
        for name in ("b", "a", "tb", "ta"):
            grouped[name] = sb.tile([P, Q * PACK], BF16, name="grouped_" + name, tag="grouped_" + name, align_bytes=64)
            nc.scalar.activation(out=words4(grouped[name][:]), in_=raw[name][:].rearrange("p j q -> p q j"), func=ACT.Copy)

        def scores(name):
            codes = sb.tile([P, Q], U32, name="codes_" + name, align_bytes=64)
            scales = sb.tile([P, Q], U8, name="scales_" + name, align_bytes=64)
            nc.vector.quantize_mx(out=codes[:].bitcast(FP8X4), scales=scales[:], in_=grouped[name][:])
            score[name] = bank("bank_" + name, "score_" + name)
            nc.tensor.matmul_mx(
                out=score[name][:],
                lhsT=codes[:].bitcast(FP8X4),
                lhsT_scale=scales[:],
                rhs=kwords[:].bitcast(FP8X4),
                rhs_scale=kscales[:],
                start=True,
                stop=True,
            )

        scores("b")
        scores("a")
        scores("tb")
        copies = sb.tile([P, 2, I], F32, name="copies", tag="grouped_tb", align_bytes=64)
        neg_b, copy_a = copies[:, 0, :], copies[:, 1, :]
        neg_max_b = col("neg_max_b")
        nc.vector.tensor_scalar(planes(neg_b), dealt(score["b"][:]), -1.0, None, ALU.mult, ALU.min, accum_out=neg_max_b[:])
        pb, sum_b = wide("pb", "raw_ta"), col("sum_b")
        nc.scalar.activation(out=planes(pb[:]), in_=dealt(score["b"][:]), func=ACT.Exp, bias=neg_max_b[:], accum_out=sum_b[:])
        scores("ta")
        max_a, neg_max_a = col("max_a"), col("neg_max_a")
        nc.vector.tensor_scalar(planes(copy_a), dealt(score["a"][:]), 1.0, None, ALU.mult, ALU.max, accum_out=max_a[:])
        nc.vector.tensor_scalar(neg_max_a[:], max_a[:], -1.0, None, ALU.mult)
        pa, sum_a = wide("pa", "then_values1"), col("sum_a")
        nc.scalar.activation(out=pa[:], in_=score["a"][:], func=ACT.Exp, bias=neg_max_a[:], accum_out=sum_a[:])

        shift1, rb, guess_b, guess_b_half, ra = col("shift1"), col("rb"), col("guess_b"), col("guess_b_half"), col("ra")
        nc.vector.reciprocal(rb[:], sum_b[:])
        nc.vector.tensor_scalar(guess_b[:], sum_b[:].bitcast(I32), LN_PER_BIT, None, ALU.mult)
        nc.vector.tensor_scalar(guess_b_half[:], sum_b[:].bitcast(I32), LN_PER_BIT, -0.5, ALU.mult, ALU.add)
        nc.vector.tensor_scalar(shift1[:], neg_max_a[:], neg_max_b[:], 0.5, ALU.subtract, ALU.subtract)
        prod_b, tsum_b = wide("prod_b"), col("tsum_b")
        nc.vector.scalar_tensor_tensor(
            planes(prod_b[:]), dealt(score["tb"][:]), 1.0, planes(pb[:]), ALU.mult, ALU.mult, accum_out=tsum_b[:]
        )
        neg_rb, neg_rb2, ra_rb = col("neg_rb"), col("neg_rb2"), col("ra_rb")
        nc.vector.tensor_scalar(neg_rb2[:], rb[:], rb[:], -1.0, ALU.mult, ALU.mult)
        nc.vector.tensor_scalar(neg_rb[:], rb[:], -1.0, None, ALU.mult)
        nc.vector.reciprocal(ra[:], sum_a[:])
        prod_a, tsum_a = wide("prod_a", "then_values0"), col("tsum_a")
        nc.vector.scalar_tensor_tensor(prod_a[:], score["ta"][:], 1.0, pa[:], ALU.mult, ALU.mult, accum_out=tsum_a[:])
        nc.vector.tensor_scalar(ra_rb[:], ra[:], rb[:], None, ALU.mult)

        ratio, square2 = col("ratio"), col("square2")
        e1, z0_half, square, z0_shift, e2, z1_shift, row_shift = (
            col("e1"), col("z0_half"), col("square"), col("z0_shift"), col("e2"), col("z1_shift"), col("row_shift"))
        bits = sum_a[:].bitcast(U32)
        nc.scalar.activation(out=e1[:], in_=bits, func=ACT.Exp, scale=-LN_PER_BIT, bias=guess_b[:])
        nc.scalar.activation(out=ratio[:], in_=sum_a[:], func=ACT.Copy, scale=rb[:])
        nc.scalar.activation(out=z0_half[:], in_=bits, func=ACT.Identity, scale=-LN_PER_BIT, bias=guess_b_half[:])
        nc.scalar.activation(out=square[:], in_=e1[:], func=ACT.Square, scale=ratio[:], bias=minus_two[:])
        nc.scalar.activation(out=z0_shift[:], in_=z0_half[:], func=ACT.Identity, bias=shift1[:])
        nc.scalar.activation(out=e2[:], in_=square[:], func=ACT.Exp, scale=0.5, bias=z0_half[:])
        nc.scalar.activation(out=z1_shift[:], in_=square[:], func=ACT.Identity, scale=0.5, bias=z0_shift[:])
        nc.scalar.activation(out=square2[:], in_=e2[:], func=ACT.Square, scale=ratio[:], bias=minus_two[:])
        nc.scalar.activation(out=row_shift[:], in_=square2[:], func=ACT.Identity, scale=0.5, bias=z1_shift[:])

        v, neg_u, bias_v, bias_u = wide("v"), wide("neg_u"), col("bias_v"), col("bias_u")
        nc.scalar.activation(out=bias_v[:], in_=tsum_b[:], func=ACT.Copy, scale=neg_rb2[:])
        nc.scalar.activation(out=bias_u[:], in_=tsum_a[:], func=ACT.Copy, scale=ra_rb[:])
        nc.scalar.activation(out=planes(v[:]), in_=dealt(score["tb"][:]), func=ACT.Identity, scale=rb[:], bias=bias_v[:])
        nc.scalar.activation(out=planes(neg_u[:]), in_=dealt(score["ta"][:]), func=ACT.Identity, scale=neg_rb[:], bias=bias_u[:])

        pb_t = bank("bank_b", "pb_t")
        turn(pb_t, plane(pb), True, True)
        logit_t = bank("bank_a", "logit_t")
        turn(logit_t, plane(neg_b), True, False)
        turn(logit_t, plane(copy_a), False, False)
        turn(logit_t, lambda r: row_shift[:, 0:1].to_broadcast([P, P]), False, True)
        diff_t = bank("bank_diff", "diff_t")
        turn(diff_t, plane(v), True, False)
        turn(diff_t, plane(neg_u), False, True)
        neg_u_t = bank("bank_u", "neg_u_t")
        turn(neg_u_t, plane(neg_u), True, True)

        def gather_values(j, tag):
            picked = sb.tile([P, I], BF16, name="picked%d" % j, tag=tag, align_bytes=64)
            nc.vector.tensor_copy(picked[:], vpool[j][:].indirect(offsets[:]))
            return picked

        def turn_values(blocks, tag):
            n = len(blocks)
            turned = ps.tile([P, n, 2, P], F32, tag=tag, name="turned")
            for k, picked in enumerate(blocks):
                pairs = picked[:].bitcast(F32)
                for u in range(2):
                    nc.tensor.transpose(turned[:, k, u, :], pairs[:, u : I // 2 : 2], ident[:])
            grouped_v = sb.tile([P, n * P * PACK], BF16, name="grouped_" + tag, align_bytes=64)
            nc.scalar.copy(
                out=grouped_v[:].bitcast(F32).rearrange("s (k e u) -> s k e u", k=n, u=2),
                in_=turned[:].rearrange("s k u e -> s k e u"),
            )
            return grouped_v

        def quantise(grouped, codes, scales):
            nc.vector.quantize_mx(out=codes.bitcast(FP8X4), scales=scales, in_=grouped[:])

        def mx_tiles(name, width):
            return (
                sb.tile([P, width], U32, name="codes_" + name, align_bytes=64),
                sb.tile([P, width], U8, name="scales_" + name, align_bytes=64),
            )

        picked0 = gather_values(0, "then_values0")
        picked1 = gather_values(1, "then_values1")
        picked2 = gather_values(2, "pool1")

        share = wide("share")
        nc.scalar.activation(out=words4(share[:]), in_=woven(logit_t[:]), func=ACT.Sigmoid)
        share_os = wide("share_os", "then_values3")
        for r in range(PACK):
            nc.scalar.activation(
                out=plane(share_os)(r), in_=words4(share[:])[:, :, r], func=ACT.Copy, scale=os_cols[:, r : r + 1]
            )
        g01 = turn_values([picked0, picked1], "bank_a")
        mix, change, harmonic = wide("mix", "pool2"), wide("change"), wide("harmonic")
        nc.vector.tensor_tensor(words4(mix[:]), woven(diff_t[:]), words4(share[:]), ALU.mult)
        g2 = turn_values([picked2], "bank_diff")
        nc.vector.tensor_tensor(words4(change[:]), words4(mix[:]), woven(neg_u_t[:]), ALU.subtract)
        nc.vector.tensor_tensor(words4(harmonic[:]), woven(pb_t[:]), woven(share_os[:]), ALU.mult)
        g3 = turn_values([gather_values(3, "then_values3")], "bank_u")
        vmx = [mx_tiles("v01", 2 * P), mx_tiles("v2", P), mx_tiles("v3", P)]
        wcodes, wscales = mx_tiles("w", Q)
        quantise(g01, vmx[0][0][:], vmx[0][1][:])
        quantise(g2, vmx[1][0][:], vmx[1][1][:])
        weights = sb.tile([P, Q * PACK], BF16, name="weights", tag="pool3", align_bytes=64)
        nc.vector.tensor_tensor(weights[:], change[:], harmonic[:], ALU.mult)
        quantise(g3, vmx[2][0][:], vmx[2][1][:])
        quantise(weights, wcodes[:], wscales[:])

        def product(acc, codes, scales):
            nc.tensor.matmul_mx(
                out=acc,
                lhsT=wcodes[:].bitcast(FP8X4),
                lhsT_scale=wscales[:],
                rhs=codes[:].bitcast(FP8X4),
                rhs_scale=scales[:],
                start=True,
                stop=True,
            )

        acc_first = bank("bank_tb", "acc_first")
        product(acc_first[:, 0 : 2 * P], *vmx[0])
        product(acc_first[:, 2 * P : 3 * P], *vmx[1])
        result_first = sb.tile([P, 3 * P], F32, name="result_first")
        nc.scalar.copy(out=result_first[:], in_=acc_first[:, 0 : 3 * P])
        nc.scalar.dma_start(out=out[:, 0 : 3 * P], in_=result_first[:])
        acc_last = bank("bank_ta", "acc_last")
        product(acc_last[:, 0:P], *vmx[2])
        result_last = sb.tile([P, P], F32, name="result_last")
        nc.vector.tensor_copy(out=result_last[:], in_=acc_last[:, 0:P])
        nc.sync.dma_start(out=out[:, 3 * P : 4 * P], in_=result_last[:])
